import numpy as np, ml_dtypes
CORES = [1,5,17,21,33,37,49,53]
N = 8
BF = ml_dtypes.bfloat16
def gentries(a):
    return np.ascontiguousarray(a.reshape(8, 16, -1).transpose(0, 2, 1)).reshape(8, -1)
def gtable(e):
    e = np.asarray(e); return np.ascontiguousarray(e.reshape(8, -1, 16).transpose(0, 2, 1)).reshape(128, -1).astype(np.int32)
W, K, F, O, C, V = 3072, 704, 1, 6, 12, 250
def pick(a, ix):
    return np.take_along_axis(a, ix[:, None, :], 2)
def draw_lists(rng):
    return rng.permuted(np.tile(np.arange(W, dtype=np.int64), (N, 8, N, F, O, 1)), axis=-1)[..., :K].copy()
def frames(rng, T, L, share):
    o = rng.integers(0, O, (N, 8, N, F)); B = np.zeros((N, 8, 16, N, F, K), np.int64)
    for r in range(N):
        for q in range(N):
            for f in range(F):
                v = pick(T[q], L[r, np.arange(8), q, f, o[r, :, q, f]]) + rng.integers(-10, 11, (8, 16, K))
                m = rng.random((8, 16, K)) < share[r, :, q, f][:, None, None]
                B[r, :, :, q, f] = np.clip(np.where(m, v, rng.integers(-V, V + 1, (8, 16, K))), -V, V)
    return B
def pack(R, B, L):
    return {"ref0": np.ascontiguousarray(R.reshape(N, 128, W)).astype(np.float32).astype(BF), "obs": np.ascontiguousarray(B.reshape(N, 128, N * F * K)).astype(np.float32).astype(BF),
            "ops": np.stack([gtable(a.reshape(8, -1)) for a in L])}
def setup_inputs(rng):
    T = rng.integers(-200, 201, (N, 8, 16, W)); R = T + rng.integers(-40, 41, T.shape); L = draw_lists(rng)
    share = rng.choice(np.array([1.0, 0.3, 0.02, 0.0]), (N, 8, N, F))
    return pack(R, frames(rng, T, L, share), L)
def setup_inputs_chain(rng):
    R = rng.integers(-200, 201, (N, 8, 16, W)); L = draw_lists(rng); B = np.zeros((N, 8, 16, N, F, K), np.int64)
    for q in range(N):
        for g in range(8):
            c = rng.permutation(W); P, Q = c[:K], c[K:2 * K]; R[q, g][:, Q] = R[q, g][:, P]
            away = rng.integers(1, 51, (16, K)) * (2 * rng.integers(0, 2, (16, K)) - 1)
            for r in range(N):
                for f in range(F):
                    z = rng.permutation(K); o = rng.permutation(O); e = 1 if rng.random() < 0.7 else -1
                    L[r, g, q, f, o[0]] = P[z]; L[r, g, q, f, o[1]] = Q[z]
                    B[r, g, :, q, f] = (R[q, g][:, P] + e * away)[:, z]
    return pack(R, B, L)
def setup_inputs_edges(rng):
    R = rng.integers(-200, 201, (N, 8, 16, W)); L = draw_lists(rng); B = np.zeros((N, 8, 16, N, F, K), np.int64)
    o = rng.integers(0, O, (N, 8, N, F)); same = rng.random((N, 8, N, F)) < 0.3
    for q in range(N):
        same[q, 0, q, 0] = True; same[q, 1, q, 0] = False
        for r in range(N):
            for f in range(F):
                s = rng.choice(np.array([0, 1, C - 1, C, C + 1, 2 * C]), (8, 16, K)) * (2 * rng.integers(0, 2, (8, 16, K)) - 1)
                B[r, :, :, q, f] = pick(R[q], L[r, np.arange(8), q, f, o[r, :, q, f]]) + np.where(same[r, :, q, f][:, None, None], 0, s)
    return pack(R, B, L)
def setup_inputs_ends(rng):
    R = rng.integers(10, V + 1, (N, 8, 16, W)); L = draw_lists(rng); B = rng.choice(np.array([-V, 1 - V, -1, 0, 1, V - 1, V]), (N, 8, 16, N, F, K))
    runs = [np.arange(K), np.arange(W - K, W), np.arange(K)[::-1], np.arange(W - 1, W - 1 - K, -1), np.arange(K) * (W // K)]
    z = rng.permuted(np.tile(np.arange(8), (N, 1)), axis=1)
    for q in range(N):
        for g in range(8):
            s = 2 * int(rng.integers(0, 2)) - 1; k = int(z[q, g])
            for r in range(N):
                for f in range(F):
                    for o in range(O):
                        i = int(rng.integers(0, len(runs) + 1))
                        L[r, g, q, f, o] = runs[i] if i < len(runs) else np.concatenate([[W - 1], 1 + rng.permutation(W - 2)[:K - 2], [0]])
            if k < 4: R[q, g] = rng.integers(V - 1 if k < 2 else 200, V + 1, (16, W))
            c = rng.permutation(W)
            for t in range(N * F if k % 2 == 1 else 1):
                r, f = (q + t // F) % N, t % F; p1, p2 = c[K - 1 + 2 * t], c[K + 2 * t]
                i = int(rng.integers(0, 16)); a = 259 + (k // 2) % 2 + 4 * int(rng.integers(0, 59)) - V
                R[q, g][:, p2] = R[q, g][:, p1]; R[q, g, i, p1] = a; R[q, g, i, p2] = a + 1
                near = np.append(c[:K - 1], p1); far = np.append(c[:K - 1], p2)
                w = int(rng.integers(1, O))
                if k == 0:
                    w = 1 + 3 * int(rng.integers(0, (O + 1) // 3))
                    if int(np.sum(R[q, g][:, near] + V)) % 2 == 1: R[q, g, 0, c[0]] = 2 * V - 1 - R[q, g, 0, c[0]]
                if k in (2, 3): w = 1 + 2 * int(rng.integers(0, O // 2))
                B[r, g, :, q, f] = -s * V
                for o in range(O): L[r, g, q, f, o] = rng.permutation(near if o == w else far)
            R[q, g] = s * R[q, g]
    return pack(R, B, L)
def setup_inputs_ties(rng):
    s = 2 * rng.integers(0, 2, (N, 8, 16, 1)) - 1; m = rng.integers(N * F * C - V, V - 2 * C, (N, 8, 16, 1))
    R = m + rng.integers(C, 2 * C + 1, (N, 8, 16, W)); R[..., W - 1] = V
    L = np.zeros((N, 8, N, F, O, K), np.int64); B = np.zeros((N, 8, 16, N, F, K), np.int64)
    for q in range(N):
        for g in range(8):
            S = rng.permutation(W - 1)[:K]
            for t in range(N * F):
                r, f = (q + t // F) % N, t % F
                if rng.random() < 0.5: S = rng.permutation(W - 1)[:K]
                w = int(rng.integers(0, O))
                for o in range(O):
                    p = rng.permutation(S)
                    if o < w or (o > w and rng.random() < 0.5): p[rng.integers(0, K)] = W - 1
                    L[r, g, q, f, o] = p
                B[r, g, :, q, f] = s[q, g] * (m[q, g] - t * C + rng.integers(0, C + 1, (16, K)))
    return pack(R * s, B, L)
def setup_inputs_spread(rng):
    z = np.exp2(-rng.integers(0, 9, (N, 8, 1, W)).astype(np.float64))
    T = (rng.integers(-V, V + 1, (N, 8, 16, W)) * z).astype(np.int64); R = np.clip(T + (rng.integers(-60, 61, T.shape) * z).astype(np.int64), -V, V); L = draw_lists(rng)
    share = rng.choice(np.array([1.0, 0.6, 0.1, 0.02, 0.0]), (N, 8, N, F))
    return pack(R, frames(rng, T, L, share), L)
def check_inputs(d):
    bad = []
    for k in ("ref0", "obs"):
        v = np.asarray(d[k]).astype(np.float32)
        if not (np.all(np.abs(v) <= V) and np.all(v == np.rint(v))): bad.append("range of " + k)
    if np.min(d["ops"]) < 0 or np.max(d["ops"]) > W - 1: bad.append("range of ops")
    for a in d["ops"]:
        e = np.sort(gentries(a).reshape(8, -1, K), axis=-1)
        if np.any(e[..., 1:] == e[..., :-1]):
            bad.append("repeated number in a list of ops"); break
    return bad
def reference(ref0, obs, ops):
    R = ref0.astype(np.float32).astype(np.int32).reshape(N, 8, 16, W); x = obs.astype(np.float32).astype(np.int32).reshape(N, 8, 16, N, F, K)
    L = np.stack([gentries(a) for a in ops]).astype(np.int64).reshape(N, 8, N, F, O, K)
    g, i = np.arange(8)[:, None, None], np.arange(16)[None, :, None]
    for q in range(N):
        for d in range(N):
            r = (q + d) % N
            for f in range(F):
                b = x[r, :, :, q, f]
                cost = np.stack([np.sum(np.abs(b - pick(R[q], L[r, :, q, f, o])), axis=(1, 2)) for o in range(O)])
                win = np.argmin(cost, axis=0)
                ix = L[r, np.arange(8), q, f, win]
                v = pick(R[q], ix)
                R[q][g, i, ix[:, None, :]] = v + np.clip(b - v, -C, C)
    return {"y": R.reshape(N, 128, W).astype(np.float32).astype(BF)}

@@ -1,0 +1,268 @@
+from concourse.mybir import AluOpType, AxisListType, ActivationFunctionType
+
+N = 8
+W, K, O, C = 3072, 704, 6, 12
+KL = K // 16
+LW = O * KL
+CH, NCH = 120, 6
+KP = CH * NCH
+V3 = 12
+A1, A2 = 12, 24
+BIG = float(2 ** 24)
+NZ = 3 + 24
+
+SCRATCH = {
+    "R": ("sbuf", [128, W], "bfloat16"),
+    "B": ("sbuf", [128, N * K], "bfloat16"),
+    "L32": ("sbuf", [128, N * LW], "int32"),
+    "L16": ("sbuf", [128, N * LW], "uint16"),
+    "SB": ("sbuf", [128, (N - 1) * K], "bfloat16"),
+    "SL": ("sbuf", [128, (N - 1) * LW], "int32"),
+    "D": ("sbuf", [128, 3 * KP], "float16"),
+    "P": ("sbuf", [128, 3 * KP], "float16"),
+    "RG": ("sbuf", [128, 3 * K], "bfloat16"),
+    "JK": ("sbuf", [128, 3 * K], "bfloat16"),
+    "RW": ("sbuf", [128, K], "bfloat16"),
+    "CL": ("sbuf", [128, K], "bfloat16"),
+    "LWN": ("sbuf", [128, 48], "uint16"),
+    "OFS": ("sbuf", [128, 4], "uint16"),
+    "AS": ("sbuf", [128, 4], "float32"),
+    "XS": ("sbuf", [128, 24], "float32"),
+    "MN": ("sbuf", [128, 4], "float32"),
+    "E": ("sbuf", [128, 28], "float32"),
+    "SC": ("sbuf", [128, 28], "float32"),
+    "WT": ("sbuf", [128, 28], "float32"),
+    "ID": ("sbuf", [128, 128], "bfloat16"),
+    "NID": ("sbuf", [128, 128], "bfloat16"),
+    "BD": ("sbuf", [128, 128], "float32"),
+    "L2": ("sbuf", [128, 128], "float32"),
+    "RD": ("sbuf", [128, 40], "float16"),
+    "RP": ("sbuf", [128, 40], "float16"),
+    "V128": ("sbuf", [128, 128], "float32"),
+    "G1": ("sbuf", [128, 128], "float32"),
+    "G40": ("sbuf", [128, 40], "float32"),
+    "G24": ("sbuf", [128, 24], "float32"),
+    "U3": ("sbuf", [128, 4], "float32"),
+    "BASE": ("sbuf", [128, 4], "float32"),
+    "PI": ("sbuf", [128, 4], "int32"),
+    "PJ": ("sbuf", [128, 4], "int32"),
+    "GP": ("sbuf", [128, 4], "float32"),
+    "PS5": ("psum", [128, 1024], "float32"),
+    "PS4": ("psum", [128, 1024], "float32"),
+    "PS3": ("psum", [128, 1024], "float32"),
+    "PXZ": ("psum", [128, 512], "float32"),
+    "PA": ("psum", [128, 512], "float32"),
+}
+SEMAPHORES = (["cv", "cs", "ct", "cg", "ldR", "ldL0", "ldB0", "stored"]
+              + ["ldL%d" % d for d in range(1, N)] + ["ldB%d" % d for d in range(1, N)]
+              + ["arL%d" % d for d in range(1, N)] + ["arB%d" % d for d in range(1, N)]
+              + ["sent%d" % d for d in range(1, N)])
+
+
+def make_tracker():
+    ops, last_w, readers, bank = [], {}, {}, {}
+    clock = {q: {} for q in ("v", "s", "t", "g", "y")}
+    count = {q: 0 for q in clock}
+    evclock = {}
+
+    def external(res, sem, val):
+        last_w[res] = (sem, val)
+        evclock[(sem, val)] = {sem: val}
+
+    def op(q, fn, r=(), w=(), banks=()):
+        deps = []
+        for x in r:
+            if x in last_w: deps.append(last_w[x])
+        for x in w:
+            if x in last_w: deps.append(last_w[x])
+            deps += readers.get(x, [])
+        for x in banks:
+            deps += [e for e in bank.get(x, {}).values() if e[0] != q]
+        waits = []
+        for e in sorted(set(deps), key=lambda e: -e[1]):
+            if q == "t" and e[0] == "t": continue
+            if clock[q].get(e[0], 0) >= e[1]: continue
+            waits.append(e)
+            for k2, v2 in evclock[e].items():
+                clock[q][k2] = max(clock[q].get(k2, 0), v2)
+        count[q] += 1
+        ev = (q, count[q])
+        c = dict(clock[q]); c[q] = count[q]
+        evclock[ev] = c
+        for x in r: readers.setdefault(x, []).append(ev)
+        for x in w:
+            last_w[x] = ev; readers[x] = []
+        for x in banks: bank.setdefault(x, {})[q] = ev
+        ops.append((q, fn, waits, ev))
+
+    def emit(queues, T):
+        need = {}
+        for q, fn, waits, ev in ops:
+            for e in waits:
+                if e[0] in count: need.setdefault(e[0], set()).add(e[1])
+        rank = {q: {i: n + 1 for n, i in enumerate(sorted(s))} for q, s in need.items()}
+        for q, fn, waits, ev in ops:
+            for e in waits:
+                if e[0] in count: queues[q].wait_ge(T.sem["c" + e[0]], rank[e[0]][e[1]])
+                else: queues[q].wait_ge(T.sem[e[0]], e[1])
+            ins = fn()
+            if ev[1] in rank.get(q, {}): ins.then_inc(T.sem["c" + q], 1)
+
+    return op, external, emit
+
+
+def rank_program(g, core, T, topo):
+    rank = T.rank_of(core)
+    if rank is None:
+        return
+    alu, act = AluOpType, ActivationFunctionType
+    V, S, PE, Y = g.vector, g.scalar, g.tensor, g.sync
+    sem = T.sem
+    op, external, emit = make_tracker()
+
+    Y.dma_start(T.R[:], T.ref0[:]).then_inc(sem.ldR, 16)
+    S.dma_start(T.L32[:, 0:LW], T.ops[:, rank * LW:(rank + 1) * LW]).then_inc(sem.ldL0, 16)
+    S.dma_start(T.B[:, 0:K], T.obs[:, rank * K:(rank + 1) * K]).then_inc(sem.ldB0, 16)
+    external("R", "ldR", 16); external("L32_0", "ldL0", 16); external("B0", "ldB0", 16)
+    dst = {d: T.cores[(rank - d) % N] for d in range(1, N)}
+    src = {d: T.cores[(rank + d) % N] for d in range(1, N)}
+    for d in range(1, N):
+        q = (rank - d) % N
+        if d == 2:
+            Y.wait_ge(sem.ldL1, 16); Y.wait_ge(sem.ldB1, 16)
+        elif d > 2:
+            Y.wait_ge(sem["sent%d" % (d - 2)], 2 * len(topo.engines(core, dst[d - 2])))
+        Y.dma_start(T.SL[:, (d - 1) * LW:d * LW], T.ops[:, q * LW:(q + 1) * LW]).then_inc(sem["ldL%d" % d], 16)
+        Y.dma_start(T.SB[:, (d - 1) * K:d * K], T.obs[:, q * K:(q + 1) * K]).then_inc(sem["ldB%d" % d], 16)
+        n_in = len(topo.engines(src[d], core))
+        external("L32_%d" % d, "arL%d" % d, n_in); external("B%d" % d, "arB%d" % d, n_in)
+
+    f = dict(allow_small_or_imprecise_dtypes=True)
+    op("g", lambda: g.iota(T.V128[:], [[-1, 128]], 0, 1, **f), w=["V128"])
+    op("g", lambda: g.iota(T.PI[:], [[0, 4]], 0, 1), w=["PI"])
+    op("g", lambda: g.iota(T.G40[:], [[1, 40]], -16, 0, **f), w=["G40"])
+    op("g", lambda: g.iota(T.G24[:], [[0, 3], [1, 8]], 0, 0, **f), w=["G24"])
+    op("g", lambda: g.iota(T.G1[:], [[1, 8], [0, 16]], 0, 0, **f), w=["G1"])
+    op("g", lambda: g.iota(T.U3[:], [[16, 4]], 0, 1, **f), w=["U3"])
+    gp, gp16, low, km = T.GP[:, 0:1], T.GP[:, 1:2], T.GP[:, 2:3], T.V128[:, CH:CH + 1]
+    op("v", lambda: V.tensor_scalar(T.ID[:], T.V128[:], 0.0, None, alu.is_equal), r=["V128"], w=["ID"])
+    op("v", lambda: V.tensor_scalar(T.NID[:], T.V128[:], 0.0, -1.0, alu.is_equal, alu.mult), r=["V128"], w=["NID"])
+    op("v", lambda: V.tensor_scalar(T.PJ[:], T.PI[:], 4, None, alu.arith_shift_right), r=["PI"], w=["PJ"])
+    op("v", lambda: V.tensor_scalar(low, km, 0.0, None, alu.is_lt), r=["V128"], w=["low"])
+    for buf, name in ((T.D, "D"), (T.P, "P")):
+        for o in range(3):
+            op("v", lambda buf=buf, o=o: V.tensor_scalar(buf[:, o * KP + K:(o + 1) * KP], T.V128[:, 0:KP - K], 0.0, None, alu.mult),
+               r=["V128"], w=["pad%s%d" % (name, o)])
+    op("v", lambda: V.tensor_copy(gp, T.PJ[:, 0:1]), r=["PJ"], w=["gp"])
+    op("v", lambda: V.memset(T.WT[:, 0:3], float(KL)), w=["WTa"])
+    op("v", lambda: V.tensor_scalar(T.XS[:], T.G24[:], km, BIG, alu.not_equal, alu.mult), r=["G24", "V128"], w=["XS"])
+    op("v", lambda: V.tensor_scalar(T.RD[:], T.G40[:], gp, -1.0, alu.is_equal, alu.mult), r=["G40", "gp"], w=["RD"])
+    op("v", lambda: V.tensor_scalar(T.RP[:], T.G40[:], gp, 2.0, alu.is_equal, alu.mult), r=["G40", "gp"], w=["RP"])
+    op("v", lambda: V.tensor_scalar(gp16, gp, 16.0, None, alu.mult), r=["gp"], w=["gp16"])
+    op("v", lambda: V.tensor_scalar(T.WT[:, 3:NZ], T.G24[:], gp, float(KL), alu.is_equal, alu.mult), r=["G24", "gp"], w=["WTb"])
+    op("v", lambda: V.tensor_scalar(T.BD[:], T.G1[:], gp, None, alu.is_equal), r=["G1", "gp"], w=["BD"])
+    op("v", lambda: V.tensor_scalar(T.L2[:], T.G1[:], km, low, alu.is_equal, alu.max), r=["G1", "V128", "low"], w=["L2"])
+    op("v", lambda: V.tensor_scalar(T.BASE[:], T.U3[:], gp16, None, alu.subtract), r=["U3", "gp16"], w=["BASE"])
+
+    for d in range(1, N):
+        rid, pid, _se = topo.addr(dst[d])
+        m = topo.mask(core, dst[d])
+        external("SL%d" % d, "ldL%d" % d, 16); external("SB%d" % d, "ldB%d" % d, 16)
+        op("g", lambda d=d, rid=rid, pid=pid, m=m: g.remote_dma(T.L32[:, d * LW:(d + 1) * LW], T.SL[:, (d - 1) * LW:d * LW],
+                                                              sem["arL%d" % d], sem["sent%d" % d], pid, rid, m), r=["SL%d" % d])
+        op("g", lambda d=d, rid=rid, pid=pid, m=m: g.remote_dma(T.B[:, d * K:(d + 1) * K], T.SB[:, (d - 1) * K:d * K],
+                                                              sem["arB%d" % d], sem["sent%d" % d], pid, rid, m), r=["SB%d" % d])
+
+    PS = {5: T.PS5, 4: T.PS4, 3: T.PS3}
+    RGO = {5: 0, 4: K, 3: 2 * K}
+    halves = ((0, 512), (512, K))
+    upd = [(0, 16 * A1, T.PA[:, 0:16 * A1], "bA"),
+           (16 * A2, K, T.PS3[:, 0:K - 16 * A2], "b30"),
+           (16 * A1, 16 * A2, T.PS3[:, 512:512 + 16 * (A2 - A1)], "b31")]
+    Z = T.PXZ[:, 32:32 + NZ]
+
+    def convert(d):
+        op("v", lambda: V.tensor_copy(T.L16[:, d * LW:(d + 1) * LW], T.L32[:, d * LW:(d + 1) * LW]), r=["L32_%d" % d], w=["L16_%d" % d])
+
+    def preload(d):
+        for o in (5, 4, 3):
+            for h, (a, z) in enumerate(halves):
+                op("t", lambda o=o, a=a, z=z: PE.matmul(PS[o][:, a:z], T.ID[:], T.B[:, d * K + a:d * K + z], True, False),
+                   r=["ID", "B%d" % d], w=["ps%d%d" % (o, h)], banks=["b%d%d" % (o, h)])
+
+    def meeting(d):
+        b = T.B[:, d * K:(d + 1) * K]
+        bn, ln = "B%d" % d, "L16_%d" % d
+
+        def cols(o, a, z):
+            return T.R[:, 0:W].indirect(T.L16[:, d * LW + o * KL + a:d * LW + o * KL + z])
+
+        def gsub(o):
+            op("v", lambda: V.tensor_tensor(T.D[:, o * KP:o * KP + K], cols(o, 0, KL), b, alu.subtract), r=["R", ln, bn], w=["D%d" % o])
+
+        def relu(o):
+            op("v", lambda: V.tensor_scalar(T.P[:, o * KP:o * KP + K], T.D[:, o * KP:o * KP + K], 0.0, None, alu.max), r=["D%d" % o], w=["P%d" % o])
+
+        def sgather(o, a):
+            op("s", lambda: S.activation(T.RG[:, RGO[o] + 16 * a:RGO[o] + K], cols(o, a, KL), act.Copy), r=["R", ln], w=["RG%d" % o])
+
+        def diff(o):
+            for h, (a, z) in enumerate(halves):
+                op("t", lambda a=a, z=z: PE.matmul(PS[o][:, a:z], T.NID[:], T.RG[:, RGO[o] + a:RGO[o] + z], False, True),
+                   r=["NID", "RG%d" % o] + (["RG3a"] if o == 3 else []), w=["ps%d%d" % (o, h)], banks=["b%d%d" % (o, h)])
+
+        def sabs(o):
+            op("s", lambda: S.activation(T.JK[:, RGO[o]:RGO[o] + K], PS[o][:, 0:K], act.Abs, accum_out=T.AS[:, 5 - o:6 - o]),
+               r=["ps%d0" % o, "ps%d1" % o], w=["JK%d" % o, "AS%d" % o], banks=["b%d0" % o, "b%d1" % o])
+
+        def xsum(name, o, first=False, last=False):
+            buf, rhs = (T.D, T.RD) if name == "D" else (T.P, T.RP)
+            s0 = 8 * o
+            for c in range(NCH):
+                op("t", lambda c=c: PE.matmul(T.PXZ[0:CH, 0:24], buf[:, o * KP + c * CH:o * KP + (c + 1) * CH], rhs[:, s0:s0 + 24],
+                                              first and c == 0, last and c == NCH - 1),
+                   r=["%s%d" % (name, o), "pad%s%d" % (name, o), "R" + name], w=["X"], banks=["bX"])
+
+        op("v", lambda: V.tensor_copy(T.RG[:, RGO[3]:RGO[3] + 16 * V3], cols(3, 0, V3)), r=["R", ln], w=["RG3a"])
+        sgather(5, 0); gsub(0); sgather(4, 0); gsub(1); sgather(3, V3)
+        diff(5); xsum("D", 0, first=True); diff(4); xsum("D", 1); diff(3)
+        relu(0); gsub(2); relu(1); relu(2)
+        sabs(5); sabs(4); sabs(3)
+        xsum("P", 0); xsum("D", 2); xsum("P", 1); xsum("P", 2, last=True)
+        if 0 < d < N - 1: convert(d + 1)
+        op("v", lambda: V.tensor_copy(T.XS[0:CH, :], T.PXZ[0:CH, 0:24]), r=["X"], w=["XS"], banks=["bX"])
+        op("t", lambda: PE.matmul(T.PXZ[:, 35:32 + NZ], T.L2[:], T.XS[:], True, True), r=["L2", "XS"], w=["Zb"], banks=["bX"])
+        op("t", lambda: PE.matmul(T.PXZ[:, 32:35], T.BD[:], T.AS[:, 0:3], True, True), r=["BD", "AS5", "AS4", "AS3"], w=["Za"], banks=["bX"])
+        for i, (a, z, ps, bk) in enumerate(upd):
+            op("t", lambda a=a, z=z, ps=ps: PE.matmul(ps, T.ID[:], b[:, a:z] if False else T.B[:, d * K + a:d * K + z], True, False),
+               r=["ID", bn], w=["u%d" % i] + (["ps30"] if bk == "b30" else ["ps31"] if bk == "b31" else []), banks=[bk])
+        op("v", lambda: V.tensor_reduce(T.MN[:, 0:1], Z, AxisListType.X, alu.min), r=["Za", "Zb"], w=["MN"], banks=["bX"])
+        op("v", lambda: V.tensor_scalar(T.E[:, 0:NZ], Z, T.MN[:, 0:1], None, alu.is_gt), r=["Za", "Zb", "MN"], w=["E"], banks=["bX"])
+        op("v", lambda: V.tensor_tensor_scan(T.SC[:, 0:NZ], T.WT[:, 0:NZ], T.E[:, 0:NZ], 0.0, alu.add, alu.mult), r=["WTa", "WTb", "E"], w=["SC"])
+        op("v", lambda: V.tensor_scalar(T.OFS[:, 0:3], T.BASE[:, 0:3], T.SC[:, NZ - 1:NZ], float(LW - 1), alu.add, alu.min), r=["BASE", "SC"], w=["OFS"])
+        op("v", lambda: V.tensor_copy(T.LWN[:], T.L32[:, d * LW:(d + 1) * LW].indirect(T.OFS[:, 0:3])), r=["L32_%d" % d, "OFS"], w=["LWN"])
+        def won(a, z):
+            return T.R[:, 0:W].indirect(T.LWN[:, a:z])
+        op("s", lambda: S.activation(T.RW[:, 0:16 * A1], won(0, A1), act.Copy), r=["R", "LWN"], w=["RW0"])
+        op("v", lambda: V.tensor_copy(T.RW[:, 16 * A2:K], won(A2, KL)), r=["R", "LWN"], w=["RW1"])
+        op("s", lambda: S.activation(T.RW[:, 16 * A1:16 * A2], won(A1, A2), act.Copy), r=["R", "LWN"], w=["RW2"])
+        for i, (a, z, ps, bk) in enumerate(upd):
+            op("t", lambda a=a, z=z, ps=ps: PE.matmul(ps, T.NID[:], T.RW[:, a:z], False, True), r=["NID", "RW%d" % i], w=["u%d" % i], banks=[bk])
+        for i, (a, z, ps, bk) in enumerate(upd):
+            op("v", lambda a=a, z=z, ps=ps: V.tensor_scalar(T.CL[:, a:z], ps, float(C), float(-C), alu.min, alu.max),
+               r=["u%d" % i], w=["CL%d" % i], banks=[bk])
+        op("v", lambda: V.tensor_tensor(won(0, KL), T.RW[:], T.CL[:], alu.add),
+           r=["RW0", "RW1", "RW2", "CL0", "CL1", "CL2", "LWN"], w=["R"])
+        if d == 0: convert(1)
+        if d < N - 1: preload(d + 1)
+
+    convert(0)
+    preload(0)
+    for d in range(N):
+        meeting(d)
+    op("y", lambda: Y.dma_start(T.y[:], T.R[:]).then_inc(sem.stored, 16), r=["R"])
+
+    emit({"v": V, "s": S, "t": PE, "g": g, "y": Y}, T)
+    Y.wait_ge(sem.stored, 16)
+    for d in range(N - 2, N):
+        g.wait_ge(sem["sent%d" % d], 2 * len(topo.engines(core, dst[d])))

@@ -4,34 +4,36 @@ N = 8
 W, K, O, C = 3072, 704, 6, 12
 KL = K // 16
 LW = O * KL
+LS = LW + 8
 CH, NCH = 120, 6
 KP = CH * NCH
 V3 = 12
-A1, A2 = 12, 24
+U1, U2, U3 = 12, 24, 32
+UORD = (2, 0, 3, 1)
 BIG = float(2 ** 24)
 NZ = 3 + 24
 
 SCRATCH = {
     "R": ("sbuf", [128, W], "bfloat16"),
     "B": ("sbuf", [128, N * K], "bfloat16"),
-    "L32": ("sbuf", [128, N * LW], "int32"),
+    "L32": ("sbuf", [128, N * LS], "int32"),
     "L16": ("sbuf", [128, N * LW], "uint16"),
     "SB": ("sbuf", [128, (N - 1) * K], "bfloat16"),
     "SL": ("sbuf", [128, (N - 1) * LW], "int32"),
     "D": ("sbuf", [128, 3 * KP], "float16"),
     "P": ("sbuf", [128, 3 * KP], "float16"),
+    "D3": ("sbuf", [128, 16 * V3], "float32"),
     "RG": ("sbuf", [128, 3 * K], "bfloat16"),
     "JK": ("sbuf", [128, 3 * K], "bfloat16"),
     "RW": ("sbuf", [128, K], "bfloat16"),
     "CL": ("sbuf", [128, K], "bfloat16"),
     "LWN": ("sbuf", [128, 48], "uint16"),
-    "OFS": ("sbuf", [128, 4], "uint16"),
-    "AS": ("sbuf", [128, 4], "float32"),
+    "AS": ("sbuf", [128, 8], "float32"),
     "XS": ("sbuf", [128, 24], "float32"),
     "MN": ("sbuf", [128, 4], "float32"),
-    "E": ("sbuf", [128, 28], "float32"),
-    "SC": ("sbuf", [128, 28], "float32"),
-    "WT": ("sbuf", [128, 28], "float32"),
+    "E": ("sbuf", [128, 32], "float32"),
+    "SC": ("sbuf", [128, 32], "uint16"),
+    "WT": ("sbuf", [128, 32], "float32"),
     "ID": ("sbuf", [128, 128], "bfloat16"),
     "NID": ("sbuf", [128, 128], "bfloat16"),
     "BD": ("sbuf", [128, 128], "float32"),
@@ -42,16 +44,16 @@ SCRATCH = {
     "G1": ("sbuf", [128, 128], "float32"),
     "G40": ("sbuf", [128, 40], "float32"),
     "G24": ("sbuf", [128, 24], "float32"),
-    "U3": ("sbuf", [128, 4], "float32"),
-    "BASE": ("sbuf", [128, 4], "float32"),
     "PI": ("sbuf", [128, 4], "int32"),
     "PJ": ("sbuf", [128, 4], "int32"),
+    "PK": ("sbuf", [128, 4], "int32"),
     "GP": ("sbuf", [128, 4], "float32"),
     "PS5": ("psum", [128, 1024], "float32"),
     "PS4": ("psum", [128, 1024], "float32"),
-    "PS3": ("psum", [128, 1024], "float32"),
+    "PS3": ("psum", [128, 512], "float32"),
     "PXZ": ("psum", [128, 512], "float32"),
-    "PA": ("psum", [128, 512], "float32"),
+    "PU0": ("psum", [128, 512], "float32"),
+    "PU1": ("psum", [128, 512], "float32"),
 }
 SEMAPHORES = (["cv", "cs", "ct", "cg", "ldR", "ldL0", "ldB0", "stored"]
               + ["ldL%d" % d for d in range(1, N)] + ["ldB%d" % d for d in range(1, N)]
@@ -128,9 +130,11 @@ def rank_program(g, core, T, topo):
     src = {d: T.cores[(rank + d) % N] for d in range(1, N)}
     for d in range(1, N):
         q = (rank - d) % N
-        if d == 2:
+        if d == 1:
+            Y.wait_ge(sem.ldL0, 16)
+        elif d == 2:
             Y.wait_ge(sem.ldL1, 16); Y.wait_ge(sem.ldB1, 16)
-        elif d > 2:
+        else:
             Y.wait_ge(sem["sent%d" % (d - 2)], 2 * len(topo.engines(core, dst[d - 2])))
         Y.dma_start(T.SL[:, (d - 1) * LW:d * LW], T.ops[:, q * LW:(q + 1) * LW]).then_inc(sem["ldL%d" % d], 16)
         Y.dma_start(T.SB[:, (d - 1) * K:d * K], T.obs[:, q * K:(q + 1) * K]).then_inc(sem["ldB%d" % d], 16)
@@ -143,52 +147,67 @@ def rank_program(g, core, T, topo):
     op("g", lambda: g.iota(T.G40[:], [[1, 40]], -16, 0, **f), w=["G40"])
     op("g", lambda: g.iota(T.G24[:], [[0, 3], [1, 8]], 0, 0, **f), w=["G24"])
     op("g", lambda: g.iota(T.G1[:], [[1, 8], [0, 16]], 0, 0, **f), w=["G1"])
-    op("g", lambda: g.iota(T.U3[:], [[16, 4]], 0, 1, **f), w=["U3"])
-    gp, gp16, low, km = T.GP[:, 0:1], T.GP[:, 1:2], T.GP[:, 2:3], T.V128[:, CH:CH + 1]
+    gp, low, km = T.GP[:, 0:1], T.GP[:, 2:3], T.V128[:, CH:CH + 1]
+    for d in range(N):
+        op("v", lambda d=d: V.memset(T.L32[:, d * LS + LW:(d + 1) * LS], 0), w=["padL%d" % d])
+    op("v", lambda: V.memset(T.AS[:, 4:6], 0.0), w=["AS0"])
+    op("v", lambda: V.memset(T.E[:, NZ:32], 1.0), w=["E1"])
+    for a, z, val in ((0, 3, KL), (NZ, NZ + 1, 0), (NZ + 2, 32, 16)):
+        op("v", lambda a=a, z=z, val=val: V.memset(T.WT[:, a:z], float(val)), w=["WT%d" % a])
     op("v", lambda: V.tensor_scalar(T.ID[:], T.V128[:], 0.0, None, alu.is_equal), r=["V128"], w=["ID"])
     op("v", lambda: V.tensor_scalar(T.NID[:], T.V128[:], 0.0, -1.0, alu.is_equal, alu.mult), r=["V128"], w=["NID"])
     op("v", lambda: V.tensor_scalar(T.PJ[:], T.PI[:], 4, None, alu.arith_shift_right), r=["PI"], w=["PJ"])
+    op("v", lambda: V.tensor_scalar(T.PK[:], T.PI[:], 15, None, alu.bitwise_and), r=["PI"], w=["PK"])
     op("v", lambda: V.tensor_scalar(low, km, 0.0, None, alu.is_lt), r=["V128"], w=["low"])
     for buf, name in ((T.D, "D"), (T.P, "P")):
         for o in range(3):
             op("v", lambda buf=buf, o=o: V.tensor_scalar(buf[:, o * KP + K:(o + 1) * KP], T.V128[:, 0:KP - K], 0.0, None, alu.mult),
                r=["V128"], w=["pad%s%d" % (name, o)])
     op("v", lambda: V.tensor_copy(gp, T.PJ[:, 0:1]), r=["PJ"], w=["gp"])
-    op("v", lambda: V.memset(T.WT[:, 0:3], float(KL)), w=["WTa"])
+    op("v", lambda: V.tensor_copy(T.WT[:, NZ + 1:NZ + 2], T.PK[:, 0:1]), r=["PK"], w=["WTp"])
     op("v", lambda: V.tensor_scalar(T.XS[:], T.G24[:], km, BIG, alu.not_equal, alu.mult), r=["G24", "V128"], w=["XS"])
     op("v", lambda: V.tensor_scalar(T.RD[:], T.G40[:], gp, -1.0, alu.is_equal, alu.mult), r=["G40", "gp"], w=["RD"])
     op("v", lambda: V.tensor_scalar(T.RP[:], T.G40[:], gp, 2.0, alu.is_equal, alu.mult), r=["G40", "gp"], w=["RP"])
-    op("v", lambda: V.tensor_scalar(gp16, gp, 16.0, None, alu.mult), r=["gp"], w=["gp16"])
     op("v", lambda: V.tensor_scalar(T.WT[:, 3:NZ], T.G24[:], gp, float(KL), alu.is_equal, alu.mult), r=["G24", "gp"], w=["WTb"])
     op("v", lambda: V.tensor_scalar(T.BD[:], T.G1[:], gp, None, alu.is_equal), r=["G1", "gp"], w=["BD"])
     op("v", lambda: V.tensor_scalar(T.L2[:], T.G1[:], km, low, alu.is_equal, alu.max), r=["G1", "V128", "low"], w=["L2"])
-    op("v", lambda: V.tensor_scalar(T.BASE[:], T.U3[:], gp16, None, alu.subtract), r=["U3", "gp16"], w=["BASE"])
+    WTS = ["WT0", "WT%d" % NZ, "WT%d" % (NZ + 2), "WTp", "WTb", "E1"]
 
     for d in range(1, N):
         rid, pid, _se = topo.addr(dst[d])
         m = topo.mask(core, dst[d])
         external("SL%d" % d, "ldL%d" % d, 16); external("SB%d" % d, "ldB%d" % d, 16)
-        op("g", lambda d=d, rid=rid, pid=pid, m=m: g.remote_dma(T.L32[:, d * LW:(d + 1) * LW], T.SL[:, (d - 1) * LW:d * LW],
+        op("g", lambda d=d, rid=rid, pid=pid, m=m: g.remote_dma(T.L32[:, d * LS:d * LS + LW], T.SL[:, (d - 1) * LW:d * LW],
                                                               sem["arL%d" % d], sem["sent%d" % d], pid, rid, m), r=["SL%d" % d])
         op("g", lambda d=d, rid=rid, pid=pid, m=m: g.remote_dma(T.B[:, d * K:(d + 1) * K], T.SB[:, (d - 1) * K:d * K],
                                                               sem["arB%d" % d], sem["sent%d" % d], pid, rid, m), r=["SB%d" % d])
 
-    PS = {5: T.PS5, 4: T.PS4, 3: T.PS3}
-    RGO = {5: 0, 4: K, 3: 2 * K}
-    halves = ((0, 512), (512, K))
-    upd = [(0, 16 * A1, T.PA[:, 0:16 * A1], "bA"),
-           (16 * A2, K, T.PS3[:, 0:K - 16 * A2], "b30"),
-           (16 * A1, 16 * A2, T.PS3[:, 512:512 + 16 * (A2 - A1)], "b31")]
+    SW = {5: (T.PS5, 0, 0, 0), 4: (T.PS4, K, 0, 1), 3: (T.PS3, 2 * K, 16 * V3, 6)}
+
+    def parts(o):
+        n = K - SW[o][2]
+        return [(h, a, min(a + 512, n)) for h, a in enumerate(range(0, n, 512))]
+
+    upd = [(0, U1, T.PU0, "u0", "bU0"), (U1, U2, T.PS5, "ps50", "b50"), (U2, U3, T.PU1, "u1", "bU1"), (U3, KL, T.PS4, "ps40", "b40")]
+    upd = [u for u in upd if u[1] > u[0]]
     Z = T.PXZ[:, 32:32 + NZ]
 
     def convert(d):
-        op("v", lambda: V.tensor_copy(T.L16[:, d * LW:(d + 1) * LW], T.L32[:, d * LW:(d + 1) * LW]), r=["L32_%d" % d], w=["L16_%d" % d])
+        op("v", lambda: V.tensor_copy(T.L16[:, d * LW:(d + 1) * LW], T.L32[:, d * LS:d * LS + LW]), r=["L32_%d" % d], w=["L16_%d" % d])
+
+    def lay(d, ps, n, first, name, bk):
+        op("t", lambda: PE.matmul(ps, T.ID[:], T.B[:, d * K + first:d * K + first + n], True, False), r=["ID", "B%d" % d], w=[name], banks=[bk])
+
+    def lay_upd(d, i):
+        a, z, ps, nm, bk = upd[i]
+        lay(d, ps[:, 0:16 * (z - a)], 16 * (z - a), 16 * a, nm, bk)
+
+    def lay_way(d, o):
+        for h, a, z in parts(o):
+            lay(d, SW[o][0][:, a:z], z - a, SW[o][2] + a, "ps%d%d" % (o, h), "b%d%d" % (o, h))
 
     def preload(d):
-        for o in (5, 4, 3):
-            for h, (a, z) in enumerate(halves):
-                op("t", lambda o=o, a=a, z=z: PE.matmul(PS[o][:, a:z], T.ID[:], T.B[:, d * K + a:d * K + z], True, False),
-                   r=["ID", "B%d" % d], w=["ps%d%d" % (o, h)], banks=["b%d%d" % (o, h)])
+        lay_way(d, 4); lay_way(d, 3); lay_way(d, 5); lay_upd(d, 0); lay_upd(d, 2)
 
     def meeting(d):
         b = T.B[:, d * K:(d + 1) * K]
@@ -203,17 +222,20 @@ def rank_program(g, core, T, topo):
         def relu(o):
             op("v", lambda: V.tensor_scalar(T.P[:, o * KP:o * KP + K], T.D[:, o * KP:o * KP + K], 0.0, None, alu.max), r=["D%d" % o], w=["P%d" % o])
 
-        def sgather(o, a):
-            op("s", lambda: S.activation(T.RG[:, RGO[o] + 16 * a:RGO[o] + K], cols(o, a, KL), act.Copy), r=["R", ln], w=["RG%d" % o])
+        def sgather(o):
+            ps, at, first, col = SW[o]
+            op("s", lambda: S.activation(T.RG[:, at:at + K - first], cols(o, first // 16, KL), act.Copy), r=["R", ln], w=["RG%d" % o])
 
         def diff(o):
-            for h, (a, z) in enumerate(halves):
-                op("t", lambda a=a, z=z: PE.matmul(PS[o][:, a:z], T.NID[:], T.RG[:, RGO[o] + a:RGO[o] + z], False, True),
-                   r=["NID", "RG%d" % o] + (["RG3a"] if o == 3 else []), w=["ps%d%d" % (o, h)], banks=["b%d%d" % (o, h)])
+            ps, at, first, col = SW[o]
+            for h, a, z in parts(o):
+                op("t", lambda a=a, z=z: PE.matmul(ps[:, a:z], T.NID[:], T.RG[:, at + a:at + z], False, True),
+                   r=["NID", "RG%d" % o], w=["ps%d%d" % (o, h)], banks=["b%d%d" % (o, h)])
 
         def sabs(o):
-            op("s", lambda: S.activation(T.JK[:, RGO[o]:RGO[o] + K], PS[o][:, 0:K], act.Abs, accum_out=T.AS[:, 5 - o:6 - o]),
-               r=["ps%d0" % o, "ps%d1" % o], w=["JK%d" % o, "AS%d" % o], banks=["b%d0" % o, "b%d1" % o])
+            ps, at, first, col = SW[o]
+            op("s", lambda: S.activation(T.JK[:, at:at + K - first], ps[:, 0:K - first], act.Abs, accum_out=T.AS[:, col:col + 1]),
+               r=["ps%d%d" % (o, h) for h, a, z in parts(o)], w=["JK%d" % o, "AS%d" % o], banks=["b%d%d" % (o, h) for h, a, z in parts(o)])
 
         def xsum(name, o, first=False, last=False):
             buf, rhs = (T.D, T.RD) if name == "D" else (T.P, T.RP)
@@ -223,37 +245,49 @@ def rank_program(g, core, T, topo):
                                               first and c == 0, last and c == NCH - 1),
                    r=["%s%d" % (name, o), "pad%s%d" % (name, o), "R" + name], w=["X"], banks=["bX"])
 
-        op("v", lambda: V.tensor_copy(T.RG[:, RGO[3]:RGO[3] + 16 * V3], cols(3, 0, V3)), r=["R", ln], w=["RG3a"])
-        sgather(5, 0); gsub(0); sgather(4, 0); gsub(1); sgather(3, V3)
-        diff(5); xsum("D", 0, first=True); diff(4); xsum("D", 1); diff(3)
+        sgather(5); gsub(0); sgather(4); gsub(1); sgather(3)
+        xsum("D", 0, first=True); diff(5); diff(4); xsum("D", 1)
         relu(0); gsub(2); relu(1); relu(2)
+        op("v", lambda: V.tensor_tensor(T.D3[:], cols(3, 0, V3), T.B[:, d * K:d * K + 16 * V3], alu.subtract), r=["R", ln, bn], w=["D3"])
+        xsum("P", 0); diff(3); xsum("D", 2); xsum("P", 1); xsum("P", 2, last=True)
         sabs(5); sabs(4); sabs(3)
-        xsum("P", 0); xsum("D", 2); xsum("P", 1); xsum("P", 2, last=True)
-        if 0 < d < N - 1: convert(d + 1)
         op("v", lambda: V.tensor_copy(T.XS[0:CH, :], T.PXZ[0:CH, 0:24]), r=["X"], w=["XS"], banks=["bX"])
         op("t", lambda: PE.matmul(T.PXZ[:, 35:32 + NZ], T.L2[:], T.XS[:], True, True), r=["L2", "XS"], w=["Zb"], banks=["bX"])
-        op("t", lambda: PE.matmul(T.PXZ[:, 32:35], T.BD[:], T.AS[:, 0:3], True, True), r=["BD", "AS5", "AS4", "AS3"], w=["Za"], banks=["bX"])
-        for i, (a, z, ps, bk) in enumerate(upd):
-            op("t", lambda a=a, z=z, ps=ps: PE.matmul(ps, T.ID[:], b[:, a:z] if False else T.B[:, d * K + a:d * K + z], True, False),
-               r=["ID", bn], w=["u%d" % i] + (["ps30"] if bk == "b30" else ["ps31"] if bk == "b31" else []), banks=[bk])
+        op("v", lambda: V.tensor_reduce(T.AS[:, 2:3], T.D3[:], AxisListType.X, alu.add, apply_absolute_value=True), r=["D3"], w=["AS3v"])
+        op("t", lambda: PE.matmul(T.PXZ[:, 32:35], T.BD[:], T.AS[:, 0:3], True, False), r=["BD", "AS5", "AS4", "AS3v"], w=["Za"], banks=["bX"])
+        op("t", lambda: PE.matmul(T.PXZ[:, 32:35], T.BD[:], T.AS[:, 4:7], False, True), r=["BD", "AS3", "AS0"], w=["Za"], banks=["bX"])
+        if len(upd) > 3: lay_upd(d, 3)
+        lay_upd(d, 1)
+        if 0 < d < N - 1: convert(d + 1)
         op("v", lambda: V.tensor_reduce(T.MN[:, 0:1], Z, AxisListType.X, alu.min), r=["Za", "Zb"], w=["MN"], banks=["bX"])
         op("v", lambda: V.tensor_scalar(T.E[:, 0:NZ], Z, T.MN[:, 0:1], None, alu.is_gt), r=["Za", "Zb", "MN"], w=["E"], banks=["bX"])
-        op("v", lambda: V.tensor_tensor_scan(T.SC[:, 0:NZ], T.WT[:, 0:NZ], T.E[:, 0:NZ], 0.0, alu.add, alu.mult), r=["WTa", "WTb", "E"], w=["SC"])
-        op("v", lambda: V.tensor_scalar(T.OFS[:, 0:3], T.BASE[:, 0:3], T.SC[:, NZ - 1:NZ], float(LW - 1), alu.add, alu.min), r=["BASE", "SC"], w=["OFS"])
-        op("v", lambda: V.tensor_copy(T.LWN[:], T.L32[:, d * LW:(d + 1) * LW].indirect(T.OFS[:, 0:3])), r=["L32_%d" % d, "OFS"], w=["LWN"])
+        op("v", lambda: V.tensor_tensor_scan(T.SC[:, 0:NZ + 4], T.WT[:, 0:NZ + 4], T.E[:, 0:NZ + 4], 0.0, alu.add, alu.mult), r=WTS + ["E"], w=["SC"])
+        op("v", lambda: V.tensor_copy(T.LWN[:], T.L32[:, d * LS:(d + 1) * LS].indirect(T.SC[:, NZ + 1:NZ + 4])),
+           r=["L32_%d" % d, "padL%d" % d, "SC"], w=["LWN"])
+
         def won(a, z):
             return T.R[:, 0:W].indirect(T.LWN[:, a:z])
-        op("s", lambda: S.activation(T.RW[:, 0:16 * A1], won(0, A1), act.Copy), r=["R", "LWN"], w=["RW0"])
-        op("v", lambda: V.tensor_copy(T.RW[:, 16 * A2:K], won(A2, KL)), r=["R", "LWN"], w=["RW1"])
-        op("s", lambda: S.activation(T.RW[:, 16 * A1:16 * A2], won(A1, A2), act.Copy), r=["R", "LWN"], w=["RW2"])
-        for i, (a, z, ps, bk) in enumerate(upd):
-            op("t", lambda a=a, z=z, ps=ps: PE.matmul(ps, T.NID[:], T.RW[:, a:z], False, True), r=["NID", "RW%d" % i], w=["u%d" % i], banks=[bk])
-        for i, (a, z, ps, bk) in enumerate(upd):
-            op("v", lambda a=a, z=z, ps=ps: V.tensor_scalar(T.CL[:, a:z], ps, float(C), float(-C), alu.min, alu.max),
-               r=["u%d" % i], w=["CL%d" % i], banks=[bk])
-        op("v", lambda: V.tensor_tensor(won(0, KL), T.RW[:], T.CL[:], alu.add),
-           r=["RW0", "RW1", "RW2", "CL0", "CL1", "CL2", "LWN"], w=["R"])
+
+        def piece(buf, a, z):
+            return buf[:, 16 * a:16 * z]
+
+        def sub(i):
+            a, z, ps, nm, bk = upd[i]
+            op("t", lambda: PE.matmul(piece(ps, 0, z - a), T.NID[:], piece(T.RW, a, z), False, True), r=["NID", "RW%d" % a], w=[nm], banks=[bk])
+
+        def limit(i):
+            a, z, ps, nm, bk = upd[i]
+            op("v", lambda: V.tensor_scalar(piece(T.CL, a, z), piece(ps, 0, z - a), float(-C), float(C), alu.max, alu.min), r=[nm], w=["CL%d" % a], banks=[bk])
+
+        for a, z, ps, nm, bk in upd[0:2]:
+            op("s", lambda a=a, z=z: S.activation(piece(T.RW, a, z), won(a, z), act.Copy), r=["R", "LWN"], w=["RW%d" % a])
+        for a, z, ps, nm, bk in upd[2:]:
+            op("v", lambda a=a, z=z: V.tensor_copy(piece(T.RW, a, z), won(a, z)), r=["R", "LWN"], w=["RW%d" % a])
+        for i in UORD: sub(i)
+        for i in UORD: limit(i)
         if d == 0: convert(1)
+        cuts = [u[0] for u in upd]
+        op("v", lambda: V.tensor_tensor(won(0, KL), T.RW[:], T.CL[:], alu.add), r=["RW%d" % a for a in cuts] + ["CL%d" % a for a in cuts] + ["LWN"], w=["R"])
         if d < N - 1: preload(d + 1)
 
     convert(0)

from concourse.mybir import AluOpType, AxisListType, ActivationFunctionType

N = 8
W, K, O, C = 3072, 704, 6, 12
KL = K // 16
LW = O * KL
LS = LW + 8
CH, NCH = 120, 6
KP = CH * NCH
V3 = 12
U1, U2, U3 = 12, 24, 32
UORD = (2, 0, 3, 1)
BIG = float(2 ** 24)
NZ = 3 + 24

SCRATCH = {
    "R": ("sbuf", [128, W], "bfloat16"),
    "B": ("sbuf", [128, N * K], "bfloat16"),
    "L32": ("sbuf", [128, N * LS], "int32"),
    "L16": ("sbuf", [128, N * LW], "uint16"),
    "SB": ("sbuf", [128, (N - 1) * K], "bfloat16"),
    "SL": ("sbuf", [128, (N - 1) * LW], "int32"),
    "D": ("sbuf", [128, 3 * KP], "float16"),
    "P": ("sbuf", [128, 3 * KP], "float16"),
    "D3": ("sbuf", [128, 16 * V3], "float32"),
    "RG": ("sbuf", [128, 3 * K], "bfloat16"),
    "JK": ("sbuf", [128, 3 * K], "bfloat16"),
    "RW": ("sbuf", [128, K], "bfloat16"),
    "CL": ("sbuf", [128, K], "bfloat16"),
    "LWN": ("sbuf", [128, 48], "uint16"),
    "AS": ("sbuf", [128, 8], "float32"),
    "XS": ("sbuf", [128, 24], "float32"),
    "MN": ("sbuf", [128, 4], "float32"),
    "E": ("sbuf", [128, 32], "float32"),
    "SC": ("sbuf", [128, 32], "uint16"),
    "WT": ("sbuf", [128, 32], "float32"),
    "ID": ("sbuf", [128, 128], "bfloat16"),
    "NID": ("sbuf", [128, 128], "bfloat16"),
    "BD": ("sbuf", [128, 128], "float32"),
    "L2": ("sbuf", [128, 128], "float32"),
    "RD": ("sbuf", [128, 40], "float16"),
    "RP": ("sbuf", [128, 40], "float16"),
    "V128": ("sbuf", [128, 128], "float32"),
    "G1": ("sbuf", [128, 128], "float32"),
    "G40": ("sbuf", [128, 40], "float32"),
    "G24": ("sbuf", [128, 24], "float32"),
    "PI": ("sbuf", [128, 4], "int32"),
    "PJ": ("sbuf", [128, 4], "int32"),
    "PK": ("sbuf", [128, 4], "int32"),
    "GP": ("sbuf", [128, 4], "float32"),
    "PS5": ("psum", [128, 1024], "float32"),
    "PS4": ("psum", [128, 1024], "float32"),
    "PS3": ("psum", [128, 512], "float32"),
    "PXZ": ("psum", [128, 512], "float32"),
    "PU0": ("psum", [128, 512], "float32"),
    "PU1": ("psum", [128, 512], "float32"),
}
SEMAPHORES = (["cv", "cs", "ct", "cg", "ldR", "ldL0", "ldB0", "stored"]
              + ["ldL%d" % d for d in range(1, N)] + ["ldB%d" % d for d in range(1, N)]
              + ["arL%d" % d for d in range(1, N)] + ["arB%d" % d for d in range(1, N)]
              + ["sent%d" % d for d in range(1, N)])


def make_tracker():
    ops, last_w, readers, bank = [], {}, {}, {}
    clock = {q: {} for q in ("v", "s", "t", "g", "y")}
    count = {q: 0 for q in clock}
    evclock = {}

    def external(res, sem, val):
        last_w[res] = (sem, val)
        evclock[(sem, val)] = {sem: val}

    def op(q, fn, r=(), w=(), banks=()):
        deps = []
        for x in r:
            if x in last_w: deps.append(last_w[x])
        for x in w:
            if x in last_w: deps.append(last_w[x])
            deps += readers.get(x, [])
        for x in banks:
            deps += [e for e in bank.get(x, {}).values() if e[0] != q]
        waits = []
        for e in sorted(set(deps), key=lambda e: -e[1]):
            if q == "t" and e[0] == "t": continue
            if clock[q].get(e[0], 0) >= e[1]: continue
            waits.append(e)
            for k2, v2 in evclock[e].items():
                clock[q][k2] = max(clock[q].get(k2, 0), v2)
        count[q] += 1
        ev = (q, count[q])
        c = dict(clock[q]); c[q] = count[q]
        evclock[ev] = c
        for x in r: readers.setdefault(x, []).append(ev)
        for x in w:
            last_w[x] = ev; readers[x] = []
        for x in banks: bank.setdefault(x, {})[q] = ev
        ops.append((q, fn, waits, ev))

    def emit(queues, T):
        need = {}
        for q, fn, waits, ev in ops:
            for e in waits:
                if e[0] in count: need.setdefault(e[0], set()).add(e[1])
        rank = {q: {i: n + 1 for n, i in enumerate(sorted(s))} for q, s in need.items()}
        for q, fn, waits, ev in ops:
            for e in waits:
                if e[0] in count: queues[q].wait_ge(T.sem["c" + e[0]], rank[e[0]][e[1]])
                else: queues[q].wait_ge(T.sem[e[0]], e[1])
            ins = fn()
            if ev[1] in rank.get(q, {}): ins.then_inc(T.sem["c" + q], 1)

    return op, external, emit


def rank_program(g, core, T, topo):
    rank = T.rank_of(core)
    if rank is None:
        return
    alu, act = AluOpType, ActivationFunctionType
    V, S, PE, Y = g.vector, g.scalar, g.tensor, g.sync
    sem = T.sem
    op, external, emit = make_tracker()

    Y.dma_start(T.R[:], T.ref0[:]).then_inc(sem.ldR, 16)
    S.dma_start(T.L32[:, 0:LW], T.ops[:, rank * LW:(rank + 1) * LW]).then_inc(sem.ldL0, 16)
    S.dma_start(T.B[:, 0:K], T.obs[:, rank * K:(rank + 1) * K]).then_inc(sem.ldB0, 16)
    external("R", "ldR", 16); external("L32_0", "ldL0", 16); external("B0", "ldB0", 16)
    dst = {d: T.cores[(rank - d) % N] for d in range(1, N)}
    src = {d: T.cores[(rank + d) % N] for d in range(1, N)}
    for d in range(1, N):
        q = (rank - d) % N
        if d == 1:
            Y.wait_ge(sem.ldL0, 16)
        elif d == 2:
            Y.wait_ge(sem.ldL1, 16); Y.wait_ge(sem.ldB1, 16)
        else:
            Y.wait_ge(sem["sent%d" % (d - 2)], 2 * len(topo.engines(core, dst[d - 2])))
        Y.dma_start(T.SL[:, (d - 1) * LW:d * LW], T.ops[:, q * LW:(q + 1) * LW]).then_inc(sem["ldL%d" % d], 16)
        Y.dma_start(T.SB[:, (d - 1) * K:d * K], T.obs[:, q * K:(q + 1) * K]).then_inc(sem["ldB%d" % d], 16)
        n_in = len(topo.engines(src[d], core))
        external("L32_%d" % d, "arL%d" % d, n_in); external("B%d" % d, "arB%d" % d, n_in)

    f = dict(allow_small_or_imprecise_dtypes=True)
    op("g", lambda: g.iota(T.V128[:], [[-1, 128]], 0, 1, **f), w=["V128"])
    op("g", lambda: g.iota(T.PI[:], [[0, 4]], 0, 1), w=["PI"])
    op("g", lambda: g.iota(T.G40[:], [[1, 40]], -16, 0, **f), w=["G40"])
    op("g", lambda: g.iota(T.G24[:], [[0, 3], [1, 8]], 0, 0, **f), w=["G24"])
    op("g", lambda: g.iota(T.G1[:], [[1, 8], [0, 16]], 0, 0, **f), w=["G1"])
    gp, low, km = T.GP[:, 0:1], T.GP[:, 2:3], T.V128[:, CH:CH + 1]
    for d in range(N):
        op("v", lambda d=d: V.memset(T.L32[:, d * LS + LW:(d + 1) * LS], 0), w=["padL%d" % d])
    op("v", lambda: V.memset(T.AS[:, 4:6], 0.0), w=["AS0"])
    op("v", lambda: V.memset(T.E[:, NZ:32], 1.0), w=["E1"])
    for a, z, val in ((0, 3, KL), (NZ, NZ + 1, 0), (NZ + 2, 32, 16)):
        op("v", lambda a=a, z=z, val=val: V.memset(T.WT[:, a:z], float(val)), w=["WT%d" % a])
    op("v", lambda: V.tensor_scalar(T.ID[:], T.V128[:], 0.0, None, alu.is_equal), r=["V128"], w=["ID"])
    op("v", lambda: V.tensor_scalar(T.NID[:], T.V128[:], 0.0, -1.0, alu.is_equal, alu.mult), r=["V128"], w=["NID"])
    op("v", lambda: V.tensor_scalar(T.PJ[:], T.PI[:], 4, None, alu.arith_shift_right), r=["PI"], w=["PJ"])
    op("v", lambda: V.tensor_scalar(T.PK[:], T.PI[:], 15, None, alu.bitwise_and), r=["PI"], w=["PK"])
    op("v", lambda: V.tensor_scalar(low, km, 0.0, None, alu.is_lt), r=["V128"], w=["low"])
    for buf, name in ((T.D, "D"), (T.P, "P")):
        for o in range(3):
            op("v", lambda buf=buf, o=o: V.tensor_scalar(buf[:, o * KP + K:(o + 1) * KP], T.V128[:, 0:KP - K], 0.0, None, alu.mult),
               r=["V128"], w=["pad%s%d" % (name, o)])
    op("v", lambda: V.tensor_copy(gp, T.PJ[:, 0:1]), r=["PJ"], w=["gp"])
    op("v", lambda: V.tensor_copy(T.WT[:, NZ + 1:NZ + 2], T.PK[:, 0:1]), r=["PK"], w=["WTp"])
    op("v", lambda: V.tensor_scalar(T.XS[:], T.G24[:], km, BIG, alu.not_equal, alu.mult), r=["G24", "V128"], w=["XS"])
    op("v", lambda: V.tensor_scalar(T.RD[:], T.G40[:], gp, -1.0, alu.is_equal, alu.mult), r=["G40", "gp"], w=["RD"])
    op("v", lambda: V.tensor_scalar(T.RP[:], T.G40[:], gp, 2.0, alu.is_equal, alu.mult), r=["G40", "gp"], w=["RP"])
    op("v", lambda: V.tensor_scalar(T.WT[:, 3:NZ], T.G24[:], gp, float(KL), alu.is_equal, alu.mult), r=["G24", "gp"], w=["WTb"])
    op("v", lambda: V.tensor_scalar(T.BD[:], T.G1[:], gp, None, alu.is_equal), r=["G1", "gp"], w=["BD"])
    op("v", lambda: V.tensor_scalar(T.L2[:], T.G1[:], km, low, alu.is_equal, alu.max), r=["G1", "V128", "low"], w=["L2"])
    WTS = ["WT0", "WT%d" % NZ, "WT%d" % (NZ + 2), "WTp", "WTb", "E1"]

    for d in range(1, N):
        rid, pid, _se = topo.addr(dst[d])
        m = topo.mask(core, dst[d])
        external("SL%d" % d, "ldL%d" % d, 16); external("SB%d" % d, "ldB%d" % d, 16)
        op("g", lambda d=d, rid=rid, pid=pid, m=m: g.remote_dma(T.L32[:, d * LS:d * LS + LW], T.SL[:, (d - 1) * LW:d * LW],
                                                              sem["arL%d" % d], sem["sent%d" % d], pid, rid, m), r=["SL%d" % d])
        op("g", lambda d=d, rid=rid, pid=pid, m=m: g.remote_dma(T.B[:, d * K:(d + 1) * K], T.SB[:, (d - 1) * K:d * K],
                                                              sem["arB%d" % d], sem["sent%d" % d], pid, rid, m), r=["SB%d" % d])

    SW = {5: (T.PS5, 0, 0, 0), 4: (T.PS4, K, 0, 1), 3: (T.PS3, 2 * K, 16 * V3, 6)}

    def parts(o):
        n = K - SW[o][2]
        return [(h, a, min(a + 512, n)) for h, a in enumerate(range(0, n, 512))]

    upd = [(0, U1, T.PU0, "u0", "bU0"), (U1, U2, T.PS5, "ps50", "b50"), (U2, U3, T.PU1, "u1", "bU1"), (U3, KL, T.PS4, "ps40", "b40")]
    upd = [u for u in upd if u[1] > u[0]]
    Z = T.PXZ[:, 32:32 + NZ]

    def convert(d):
        op("v", lambda: V.tensor_copy(T.L16[:, d * LW:(d + 1) * LW], T.L32[:, d * LS:d * LS + LW]), r=["L32_%d" % d], w=["L16_%d" % d])

    def lay(d, ps, n, first, name, bk):
        op("t", lambda: PE.matmul(ps, T.ID[:], T.B[:, d * K + first:d * K + first + n], True, False), r=["ID", "B%d" % d], w=[name], banks=[bk])

    def lay_upd(d, i):
        a, z, ps, nm, bk = upd[i]
        lay(d, ps[:, 0:16 * (z - a)], 16 * (z - a), 16 * a, nm, bk)

    def lay_way(d, o):
        for h, a, z in parts(o):
            lay(d, SW[o][0][:, a:z], z - a, SW[o][2] + a, "ps%d%d" % (o, h), "b%d%d" % (o, h))

    def preload(d):
        lay_way(d, 4); lay_way(d, 3); lay_way(d, 5); lay_upd(d, 0); lay_upd(d, 2)

    def meeting(d):
        b = T.B[:, d * K:(d + 1) * K]
        bn, ln = "B%d" % d, "L16_%d" % d

        def cols(o, a, z):
            return T.R[:, 0:W].indirect(T.L16[:, d * LW + o * KL + a:d * LW + o * KL + z])

        def gsub(o):
            op("v", lambda: V.tensor_tensor(T.D[:, o * KP:o * KP + K], cols(o, 0, KL), b, alu.subtract), r=["R", ln, bn], w=["D%d" % o])

        def relu(o):
            op("v", lambda: V.tensor_scalar(T.P[:, o * KP:o * KP + K], T.D[:, o * KP:o * KP + K], 0.0, None, alu.max), r=["D%d" % o], w=["P%d" % o])

        def sgather(o):
            ps, at, first, col = SW[o]
            op("s", lambda: S.activation(T.RG[:, at:at + K - first], cols(o, first // 16, KL), act.Copy), r=["R", ln], w=["RG%d" % o])

        def diff(o):
            ps, at, first, col = SW[o]
            for h, a, z in parts(o):
                op("t", lambda a=a, z=z: PE.matmul(ps[:, a:z], T.NID[:], T.RG[:, at + a:at + z], False, True),
                   r=["NID", "RG%d" % o], w=["ps%d%d" % (o, h)], banks=["b%d%d" % (o, h)])

        def sabs(o):
            ps, at, first, col = SW[o]
            op("s", lambda: S.activation(T.JK[:, at:at + K - first], ps[:, 0:K - first], act.Abs, accum_out=T.AS[:, col:col + 1]),
               r=["ps%d%d" % (o, h) for h, a, z in parts(o)], w=["JK%d" % o, "AS%d" % o], banks=["b%d%d" % (o, h) for h, a, z in parts(o)])

        def xsum(name, o, first=False, last=False):
            buf, rhs = (T.D, T.RD) if name == "D" else (T.P, T.RP)
            s0 = 8 * o
            for c in range(NCH):
                op("t", lambda c=c: PE.matmul(T.PXZ[0:CH, 0:24], buf[:, o * KP + c * CH:o * KP + (c + 1) * CH], rhs[:, s0:s0 + 24],
                                              first and c == 0, last and c == NCH - 1),
                   r=["%s%d" % (name, o), "pad%s%d" % (name, o), "R" + name], w=["X"], banks=["bX"])

        sgather(5); gsub(0); sgather(4); gsub(1); sgather(3)
        xsum("D", 0, first=True); diff(5); diff(4); xsum("D", 1)
        relu(0); gsub(2); relu(1); relu(2)
        op("v", lambda: V.tensor_tensor(T.D3[:], cols(3, 0, V3), T.B[:, d * K:d * K + 16 * V3], alu.subtract), r=["R", ln, bn], w=["D3"])
        xsum("P", 0); diff(3); xsum("D", 2); xsum("P", 1); xsum("P", 2, last=True)
        sabs(5); sabs(4); sabs(3)
        op("v", lambda: V.tensor_copy(T.XS[0:CH, :], T.PXZ[0:CH, 0:24]), r=["X"], w=["XS"], banks=["bX"])
        op("t", lambda: PE.matmul(T.PXZ[:, 35:32 + NZ], T.L2[:], T.XS[:], True, True), r=["L2", "XS"], w=["Zb"], banks=["bX"])
        op("v", lambda: V.tensor_reduce(T.AS[:, 2:3], T.D3[:], AxisListType.X, alu.add, apply_absolute_value=True), r=["D3"], w=["AS3v"])
        op("t", lambda: PE.matmul(T.PXZ[:, 32:35], T.BD[:], T.AS[:, 0:3], True, False), r=["BD", "AS5", "AS4", "AS3v"], w=["Za"], banks=["bX"])
        op("t", lambda: PE.matmul(T.PXZ[:, 32:35], T.BD[:], T.AS[:, 4:7], False, True), r=["BD", "AS3", "AS0"], w=["Za"], banks=["bX"])
        if len(upd) > 3: lay_upd(d, 3)
        lay_upd(d, 1)
        if 0 < d < N - 1: convert(d + 1)
        op("v", lambda: V.tensor_reduce(T.MN[:, 0:1], Z, AxisListType.X, alu.min), r=["Za", "Zb"], w=["MN"], banks=["bX"])
        op("v", lambda: V.tensor_scalar(T.E[:, 0:NZ], Z, T.MN[:, 0:1], None, alu.is_gt), r=["Za", "Zb", "MN"], w=["E"], banks=["bX"])
        op("v", lambda: V.tensor_tensor_scan(T.SC[:, 0:NZ + 4], T.WT[:, 0:NZ + 4], T.E[:, 0:NZ + 4], 0.0, alu.add, alu.mult), r=WTS + ["E"], w=["SC"])
        op("v", lambda: V.tensor_copy(T.LWN[:], T.L32[:, d * LS:(d + 1) * LS].indirect(T.SC[:, NZ + 1:NZ + 4])),
           r=["L32_%d" % d, "padL%d" % d, "SC"], w=["LWN"])

        def won(a, z):
            return T.R[:, 0:W].indirect(T.LWN[:, a:z])

        def piece(buf, a, z):
            return buf[:, 16 * a:16 * z]

        def sub(i):
            a, z, ps, nm, bk = upd[i]
            op("t", lambda: PE.matmul(piece(ps, 0, z - a), T.NID[:], piece(T.RW, a, z), False, True), r=["NID", "RW%d" % a], w=[nm], banks=[bk])

        def limit(i):
            a, z, ps, nm, bk = upd[i]
            op("v", lambda: V.tensor_scalar(piece(T.CL, a, z), piece(ps, 0, z - a), float(-C), float(C), alu.max, alu.min), r=[nm], w=["CL%d" % a], banks=[bk])

        for a, z, ps, nm, bk in upd[0:2]:
            op("s", lambda a=a, z=z: S.activation(piece(T.RW, a, z), won(a, z), act.Copy), r=["R", "LWN"], w=["RW%d" % a])
        for a, z, ps, nm, bk in upd[2:]:
            op("v", lambda a=a, z=z: V.tensor_copy(piece(T.RW, a, z), won(a, z)), r=["R", "LWN"], w=["RW%d" % a])
        for i in UORD: sub(i)
        for i in UORD: limit(i)
        if d == 0: convert(1)
        cuts = [u[0] for u in upd]
        op("v", lambda: V.tensor_tensor(won(0, KL), T.RW[:], T.CL[:], alu.add), r=["RW%d" % a for a in cuts] + ["CL%d" % a for a in cuts] + ["LWN"], w=["R"])
        if d < N - 1: preload(d + 1)

    convert(0)
    preload(0)
    for d in range(N):
        meeting(d)
    op("y", lambda: Y.dma_start(T.y[:], T.R[:]).then_inc(sem.stored, 16), r=["R"])

    emit({"v": V, "s": S, "t": PE, "g": g, "y": Y}, T)
    Y.wait_ge(sem.stored, 16)
    for d in range(N - 2, N):
        g.wait_ge(sem["sent%d" % d], 2 * len(topo.engines(core, dst[d])))
